import numpy as np
import ml_dtypes


def mxq(x, axis, fmt="e4m3"):
    dtype, down = {"e4m3": (ml_dtypes.float8_e4m3fn, 7), "e5m2": (ml_dtypes.float8_e5m2, 14)}[fmt]
    v = np.moveaxis(np.asarray(x, np.float32).astype(ml_dtypes.bfloat16).astype(np.float64), axis, -1)
    blocks = v.reshape(v.shape[:-1] + (-1, 32))
    amax = np.abs(blocks).max(-1, keepdims=True)
    byte = np.maximum(np.where(amax > 0, np.frexp(amax)[1] - 1 + 127, 0) - down, 1)
    scale = np.exp2(byte - 127.0)
    codes = (blocks / scale).astype(np.float32).astype(dtype).astype(np.float64)
    return np.moveaxis((codes * scale).reshape(v.shape), -1, axis)


WIDE = False


def mx_kscale(k):
    if not WIDE:
        return np.ones(k)
    levels = np.array([10, -10, 5, -5, 0])
    if k % 512:
        return np.exp2(np.random.permutation(np.resize(levels, k // 32))).repeat(32)
    a = np.empty((k // 512, 16))
    for p in range(k // 512):
        a[p, :8] = np.random.permutation(np.resize(levels, 8))
        for g in range(8):
            far = levels[np.abs(levels - a[p, g]) >= 10]
            a[p, g + 8] = far[np.random.randint(len(far))]
    return np.exp2(a.ravel()).repeat(32)


def f64(x):
    return np.asarray(x).astype(np.float64)


def striped(idx):
    return np.tile(np.asarray(idx).reshape(-1, 16).T, (8, 1)).astype(np.uint16)


def unstriped(offs):
    return offs[:16].T.reshape(-1).astype(np.int64)


E2M1 = np.array([0.0, 0.5, 1.0, 1.5, 2.0, 3.0, 4.0, 6.0, -0.0, -0.5, -1.0, -1.5, -2.0, -3.0, -4.0, -6.0])


def pack_weight(w, fmt):
    k, n = w.shape
    w = f64(np.asarray(w, np.float32).astype(ml_dtypes.bfloat16)).reshape(k // 32, 32, n)
    amax = np.abs(w).max(1)
    if fmt == "e4m3":
        byte = np.frexp(amax)[1] - 1 + 127 - 7
    else:
        mant, ex = np.frexp(amax / 6.0)
        byte = np.where(mant > 0.5, ex, ex - 1) + 127
    byte = np.clip(np.where(amax > 0, byte, 1), 1, 254)
    scaled = (w * np.exp2(127.0 - byte)[:, None, :]).reshape(k, n).astype(np.float32)
    by_word = np.ascontiguousarray(scaled.reshape(k // 512, 128, 4, n).transpose(0, 1, 3, 2))
    if fmt == "e4m3":
        words = by_word.astype(ml_dtypes.float8_e4m3fn).view(np.uint8)
    else:
        c = by_word.astype(ml_dtypes.float4_e2m1fn).view(np.uint8) & 0xF
        words = (c[..., 0::2] | (c[..., 1::2] << 4)).reshape(k // 512, 128, 2 * n)
    return np.ascontiguousarray(words), np.ascontiguousarray(byte.astype(np.uint8).reshape(k // 512, 16, n))


def unpack_weight(words, scales, fmt):
    g, _, n = scales.shape
    words = np.ascontiguousarray(words).reshape(g, 128, n, -1)
    if fmt == "e4m3":
        vals = words.view(ml_dtypes.float8_e4m3fn).astype(np.float64)
    else:
        nib = np.empty((g, 128, n, 4), np.uint8)
        nib[..., 0::2] = words & 0xF
        nib[..., 1::2] = words >> 4
        vals = E2M1[nib]
    vals = vals * np.repeat(np.exp2(scales.astype(np.float64) - 127.0), 8, axis=1)[..., None]
    return vals.transpose(0, 1, 3, 2).reshape(g * 512, n)


D, E, T, I, Q, G = 512, 512, 2048, 512, 128, 64


def setup_inputs():
    n = np.random.standard_normal
    idx = np.random.permutation(T)[:I]
    fd = mx_kscale(D)
    fi = mx_kscale(I)
    ti = np.ones(T)
    ti[idx] = fi
    keysp = pack_weight(n((D, T)) / fd[:, None], "e4m3")
    return {
        "query": (n((D, Q)) * 0.7 / np.sqrt(D) * fd[:, None]).astype(np.float32),
        "keys_words": keysp[0],
        "keys_scales": keysp[1],
        "share": (np.random.uniform(0.2, 0.8, (Q, 1))).astype(np.float32),
        "os": (np.random.uniform(4.0, 16.0, (1, I)) * fi).astype(np.float32),
        "vals": (n((E, T)) / ti).astype(np.float32),
        "offs": striped(idx),
    }


def reference(query, keys_words, keys_scales, share, os, vals, offs):
    idx = unstriped(offs)
    keysu = unpack_weight(keys_words, keys_scales, "e4m3")
    queryq = mxq(f64(query), 0, "e4m3")
    keysidxg = keysu[:, idx]
    a = queryq.T @ keysidxg
    p = np.exp(a)
    z = np.sum(p, axis=1, keepdims=True)
    s = p.reshape(Q, G, I // G).sum(axis=2)
    v1 = 1.0 / (z * f64(share) + s * (1.0 - f64(share)) * 64.0)
    vr = np.repeat(v1, I // G, axis=1)
    w = p * vr
    wo1 = w * f64(os)
    wt1 = wo1.T
    vt1 = f64(vals)[:, idx].T
    wt1q = mxq(wt1, 0, "e4m3")
    vt1q = mxq(vt1, 0, "e4m3")
    o = wt1q.T @ vt1q
    return o

@@ -1,0 +1,211 @@
+from contextlib import ExitStack
+
+import concourse.mybir as mybir
+from concourse.masks import make_identity
+
+D, E, T, I, Q, G = 512, 512, 2048, 512, 128, 64
+FLOPS = 2 * D * Q * I + 2 * I * Q * E
+
+F32 = mybir.dt.float32
+BF16 = mybir.dt.bfloat16
+I32 = mybir.dt.int32
+U32 = mybir.dt.uint32
+U16 = mybir.dt.uint16
+U8 = mybir.dt.uint8
+FP8X4 = mybir.dt.float8_e4m3fn_x4
+ALU = mybir.AluOpType
+ACT = mybir.ActivationFunctionType
+AXIS = mybir.AxisListType
+
+P = 128
+PACK = 4
+BLOCKS = E // P
+GROUP = I // G
+LIST_COLS = I // 16
+VECTOR_COLS = 20
+
+
+def tile_attend_mixednorm_kernel(tc, query, keys_words, keys_scales, share, factors, vals, offs, out):
+    nc = tc.nc
+    with ExitStack() as ctx:
+        lists = ctx.enter_context(tc.tile_pool(name="lists", bufs=1))
+        keep = ctx.enter_context(tc.tile_pool(name="keep", bufs=1))
+        psum = ctx.enter_context(tc.psum_pool(name="psum", bufs=1))
+
+        offsets = lists.tile([P, LIST_COLS], U16, name="offsets")
+        nc.sync.dma_start(offsets[:], offs)
+
+        key_scale_pool = keep.tile([P, T], U8, name="key_scale_pool", align_bytes=64)
+        nc.vector.memset(key_scale_pool[:].bitcast(I32), 0)
+
+        q_raw = keep.tile([P, PACK, Q], F32, name="q_raw")
+        nc.sync.dma_start(q_raw[:], query.rearrange("(p j) q -> p j q", j=PACK))
+        for r in range(4):
+            nc.sync.dma_start(
+                key_scale_pool[r:P:32, :].bitcast(I32), keys_scales[0, r:16:4, :].bitcast(I32)
+            )
+        key_word_pool = keep.tile([P, T], U32, name="key_word_pool", align_bytes=64)
+        nc.sync.dma_start(
+            key_word_pool[:].bitcast(I32),
+            keys_words[0].rearrange("p n t -> p (n t)").bitcast(I32),
+        )
+        val_pool = [keep.tile([P, T], F32, name=f"val_pool{b}", align_bytes=64) for b in range(BLOCKS)]
+        nc.sync.dma_start(val_pool[0][:], vals[0:P, :])
+        share_col = keep.tile([P, 1], F32, name="share_col")
+        nc.sync.dma_start(share_col[:], share)
+        slot_factor = keep.tile([P, PACK], F32, name="slot_factor")
+        nc.sync.dma_start(slot_factor[:], factors.rearrange("o (p t) -> (o p) t", t=PACK))
+        for b in range(1, BLOCKS):
+            nc.sync.dma_start(val_pool[b][:], vals[b * P : (b + 1) * P, :])
+
+        identity = keep.tile([P, P], F32, name="identity")
+        make_identity(nc, identity[:])
+
+        q_bf = keep.tile([P, Q, PACK], BF16, name="q_bf", align_bytes=64)
+        nc.vector.tensor_copy(q_bf[:], q_raw[:].rearrange("p j q -> p q j"))
+        q_codes = keep.tile([P, Q], U32, name="q_codes", align_bytes=64)
+        q_scales = keep.tile([P, Q], U8, name="q_scales", align_bytes=64)
+        key_scales = keep.tile([P, I], U8, name="key_scales", align_bytes=64)
+        nc.vector.tensor_copy(key_scales[:], key_scale_pool[:].indirect(offsets[:]))
+        nc.vector.quantize_mx(
+            out=q_codes[:].bitcast(FP8X4),
+            scales=q_scales[:],
+            in_=q_bf[:].rearrange("p q j -> p (q j)"),
+        )
+        key_words = keep.tile([P, I], U32, name="key_words", align_bytes=64)
+        scores = psum.tile([P, I], F32, name="scores")
+        for half in range(2):
+            slots = slice(half * I // 2, (half + 1) * I // 2)
+            cols = slice(half * LIST_COLS // 2, (half + 1) * LIST_COLS // 2)
+            nc.vector.tensor_copy(key_words[:, slots], key_word_pool[:].indirect(offsets[:, cols]))
+            nc.tensor.matmul_mx(
+                out=scores[:, slots],
+                lhsT=q_codes[:].bitcast(FP8X4),
+                lhsT_scale=q_scales[:],
+                rhs=key_words[:, slots].bitcast(FP8X4),
+                rhs_scale=key_scales[:, slots],
+                start=True,
+                stop=True,
+            )
+
+        neg_max = keep.tile([P, 1], F32, name="neg_max")
+        nc.vector.tensor_reduce(neg_max[:], scores[:], AXIS.X, ALU.max, negate=True)
+        group_share = keep.tile([P, 1], F32, name="group_share")
+        nc.vector.tensor_scalar(group_share[:], share_col[:], -float(G), float(G), ALU.mult, ALU.add)
+
+        expo = keep.tile([P, 2, PACK, P // 2], F32, name="expo", align_bytes=64)
+        half_sum = [keep.tile([P, 1], F32, name=f"half_sum{half}") for half in range(2)]
+        group_sum = keep.tile([P, G], F32, name="group_sum")
+        for half in range(2):
+            slots = slice(half * I // 2, (half + 1) * I // 2)
+            nc.scalar.activation(
+                expo[:, half, :, :],
+                scores[:, slots].rearrange("q (s t) -> q t s", t=PACK),
+                ACT.Exp,
+                bias=neg_max[:],
+                accum_out=half_sum[half][:],
+            )
+            nc.vector.tensor_reduce(
+                group_sum[:, half * G // 2 : (half + 1) * G // 2],
+                expo[:, half, :, :].rearrange("q t (g h) -> q g t h", h=2),
+                AXIS.XY,
+                ALU.add,
+            )
+        row_part = keep.tile([P, 1], F32, name="row_part")
+        nc.vector.tensor_scalar(
+            row_part[:], half_sum[0][:], half_sum[1][:], share_col[:], ALU.add, ALU.mult
+        )
+        mix = keep.tile([P, G], F32, name="mix")
+        nc.vector.tensor_scalar(mix[:], group_sum[:], group_share[:], row_part[:], ALU.mult, ALU.add)
+        inv_mix = keep.tile([P, G], F32, name="inv_mix")
+        nc.vector.reciprocal(inv_mix[:], mix[:])
+        weights = keep.tile([P, PACK, P], F32, name="weights", align_bytes=64)
+        weights_t = psum.tile([P, PACK, Q], F32, name="weights_t")
+        for u in range(2):
+            places = slice(2 * u, 2 * u + 2)
+            nc.vector.tensor_tensor(
+                weights[:, places, :].rearrange("q t (a g h) -> q t a g h", a=2, h=2),
+                expo[:, :, places, :].rearrange("q a t (g h) -> q t a g h", h=2),
+                inv_mix[:]
+                .rearrange("q (a g) -> q a g", a=2)
+                .unsqueeze(1)
+                .unsqueeze(4)
+                .to_broadcast([P, 2, 2, G // 2, 2]),
+                ALU.mult,
+            )
+            for t in range(2 * u, 2 * u + 2):
+                nc.tensor.transpose(weights_t[:, t, :], weights[:, t, :], identity[:])
+        w_bf = keep.tile([P, Q, PACK], BF16, name="w_bf", align_bytes=64)
+        nc.vector.tensor_tensor(
+            w_bf[:],
+            weights_t[:].rearrange("s t q -> s q t"),
+            slot_factor[:].unsqueeze(1).to_broadcast([P, Q, PACK]),
+            ALU.mult,
+        )
+        w_codes = keep.tile([P, Q], U32, name="w_codes", align_bytes=64)
+        w_scales = keep.tile([P, Q], U8, name="w_scales", align_bytes=64)
+        nc.vector.quantize_mx(
+            out=w_codes[:].bitcast(FP8X4),
+            scales=w_scales[:],
+            in_=w_bf[:].rearrange("s q t -> s (q t)"),
+        )
+
+        def pick(b):
+            picked = keep.tile([P, I], BF16, name=f"picked{b}", align_bytes=64)
+            if b < BLOCKS - 1:
+                nc.scalar.activation(picked[:], val_pool[b][:].indirect(offsets[:]), ACT.Copy)
+            else:
+                cut = 16 * VECTOR_COLS
+                nc.vector.tensor_copy(
+                    picked[:, :cut], val_pool[b][:].indirect(offsets[:, :VECTOR_COLS])
+                )
+                nc.scalar.activation(
+                    picked[:, cut:], val_pool[b][:].indirect(offsets[:, VECTOR_COLS:]), ACT.Copy
+                )
+            pairs = picked[:].bitcast(F32)
+            pairs_t = psum.tile([P, 2, P], F32, name=f"pairs_t{b}")
+            for u in range(2):
+                nc.tensor.transpose(pairs_t[:, u, :], pairs[:, u : I // 2 : 2], identity[:])
+            return pairs_t
+
+        def weave(b, pairs_t, tag, copy):
+            v_bf = keep.tile([P, P * PACK], BF16, name=f"v_bf{b}", tag=tag, align_bytes=64)
+            copy(
+                v_bf[:].bitcast(F32).rearrange("s (e u) -> s e u", u=2),
+                pairs_t[:].rearrange("s u e -> s e u"),
+            )
+            return v_bf
+
+        def product(first, v_bfs, codes_tag, bank_tag, copy):
+            n = len(v_bfs) * P
+            v_codes = keep.tile([P, n], U32, name=f"v_codes{first}", tag=codes_tag, align_bytes=64)
+            v_scales = keep.tile([P, n], U8, name=f"v_scales{first}", align_bytes=64)
+            for j, v_bf in enumerate(v_bfs):
+                nc.vector.quantize_mx(
+                    out=v_codes[:, j * P : (j + 1) * P].bitcast(FP8X4),
+                    scales=v_scales[:, j * P : (j + 1) * P],
+                    in_=v_bf[:],
+                )
+            acc = psum.tile([P, n], F32, name=f"acc{first}", tag=bank_tag)
+            nc.tensor.matmul_mx(
+                out=acc[:],
+                lhsT=w_codes[:].bitcast(FP8X4),
+                lhsT_scale=w_scales[:],
+                rhs=v_codes[:].bitcast(FP8X4),
+                rhs_scale=v_scales[:],
+                start=True,
+                stop=True,
+            )
+            result = keep.tile([P, n], F32, name=f"result{first}")
+            copy(result[:], acc[:])
+            nc.sync.dma_start(out[:, first * P : first * P + n], result[:])
+
+        v_bf0 = weave(0, pick(0), "expo", nc.vector.tensor_copy)
+        v_bf1 = weave(1, pick(1), "weights", nc.vector.tensor_copy)
+        pairs_t2 = pick(2)
+        product(0, [v_bf0, v_bf1], "w_bf", "scores", nc.scalar.copy)
+        pairs_t3 = pick(3)
+        v_bf3 = weave(3, pairs_t3, "v_bf3", nc.scalar.copy)
+        v_bf2 = weave(2, pairs_t2, "val_pool3", nc.vector.tensor_copy)
+        product(2, [v_bf2], "v_codes2", "acc2", nc.scalar.copy)
+        product(3, [v_bf3], "v_codes3", "acc3", nc.vector.tensor_copy)

@@ -22,7 +22,8 @@ PACK = 4
 BLOCKS = E // P
 GROUP = I // G
 LIST_COLS = I // 16
-VECTOR_COLS = 20
+VECTOR_COLS = 18
+KEY_HEAD = 512
 
 
 def tile_attend_mixednorm_kernel(tc, query, keys_words, keys_scales, share, factors, vals, offs, out):
@@ -30,33 +31,34 @@ def tile_attend_mixednorm_kernel(tc, query, keys_words, keys_scales, share, fact
     with ExitStack() as ctx:
         lists = ctx.enter_context(tc.tile_pool(name="lists", bufs=1))
         keep = ctx.enter_context(tc.tile_pool(name="keep", bufs=1))
+        late = ctx.enter_context(tc.tile_pool(name="late", bufs=1))
         psum = ctx.enter_context(tc.psum_pool(name="psum", bufs=1))
-
-        offsets = lists.tile([P, LIST_COLS], U16, name="offsets")
-        nc.sync.dma_start(offsets[:], offs)
 
         key_scale_pool = keep.tile([P, T], U8, name="key_scale_pool", align_bytes=64)
         nc.vector.memset(key_scale_pool[:].bitcast(I32), 0)
 
         q_raw = keep.tile([P, PACK, Q], F32, name="q_raw")
         nc.sync.dma_start(q_raw[:], query.rearrange("(p j) q -> p j q", j=PACK))
+        offsets = lists.tile([P, LIST_COLS], U16, name="offsets")
+        nc.sync.dma_start(offsets[:], offs)
+        key_word_pool = keep.tile([P, T], U32, name="key_word_pool", align_bytes=64)
+        key_rows = keys_words[0].rearrange("p n t -> p (n t)").bitcast(I32)
+        nc.sync.dma_start(key_word_pool[:, :KEY_HEAD].bitcast(I32), key_rows[:, :KEY_HEAD])
         for r in range(4):
             nc.sync.dma_start(
                 key_scale_pool[r:P:32, :].bitcast(I32), keys_scales[0, r:16:4, :].bitcast(I32)
             )
-        key_word_pool = keep.tile([P, T], U32, name="key_word_pool", align_bytes=64)
-        nc.sync.dma_start(
-            key_word_pool[:].bitcast(I32),
-            keys_words[0].rearrange("p n t -> p (n t)").bitcast(I32),
-        )
-        val_pool = [keep.tile([P, T], F32, name=f"val_pool{b}", align_bytes=64) for b in range(BLOCKS)]
-        nc.sync.dma_start(val_pool[0][:], vals[0:P, :])
-        share_col = keep.tile([P, 1], F32, name="share_col")
-        nc.sync.dma_start(share_col[:], share)
+        nc.sync.dma_start(key_word_pool[:, KEY_HEAD:].bitcast(I32), key_rows[:, KEY_HEAD:])
         slot_factor = keep.tile([P, PACK], F32, name="slot_factor")
         nc.sync.dma_start(slot_factor[:], factors.rearrange("o (p t) -> (o p) t", t=PACK))
+        val_pool = [keep.tile([P, T], F32, name=f"val_pool{b}") for b in range(BLOCKS - 1)]
+        val_pool.append(late.tile([P, T], F32, name="val_pool_last", align_bytes=64, offset=0))
+        nc.sync.dma_start(val_pool[0][:], vals[0:P, :])
+
         for b in range(1, BLOCKS):
             nc.sync.dma_start(val_pool[b][:], vals[b * P : (b + 1) * P, :])
+        share_col = keep.tile([P, 1], F32, name="share_col")
+        nc.gpsimd.dma_start(share_col[:], share)
 
         identity = keep.tile([P, P], F32, name="identity")
         make_identity(nc, identity[:])
@@ -73,13 +75,13 @@ def tile_attend_mixednorm_kernel(tc, query, keys_words, keys_scales, share, fact
             in_=q_bf[:].rearrange("p q j -> p (q j)"),
         )
         key_words = keep.tile([P, I], U32, name="key_words", align_bytes=64)
-        scores = psum.tile([P, I], F32, name="scores")
+        scores = [psum.tile([P, I // 2], F32, name=f"scores{half}", tag=f"acc{half}") for half in range(2)]
         for half in range(2):
             slots = slice(half * I // 2, (half + 1) * I // 2)
             cols = slice(half * LIST_COLS // 2, (half + 1) * LIST_COLS // 2)
             nc.vector.tensor_copy(key_words[:, slots], key_word_pool[:].indirect(offsets[:, cols]))
             nc.tensor.matmul_mx(
-                out=scores[:, slots],
+                out=scores[half][:],
                 lhsT=q_codes[:].bitcast(FP8X4),
                 lhsT_scale=q_scales[:],
                 rhs=key_words[:, slots].bitcast(FP8X4),
@@ -87,54 +89,73 @@ def tile_attend_mixednorm_kernel(tc, query, keys_words, keys_scales, share, fact
                 start=True,
                 stop=True,
             )
+        dealt = [scores[half][:].rearrange("q (s t) -> q t s", t=PACK) for half in range(2)]
 
+        neg_max_first = keep.tile([P, 1], F32, name="neg_max_first")
+        nc.vector.tensor_reduce(neg_max_first[:], scores[0][:], AXIS.X, ALU.max, negate=True)
         neg_max = keep.tile([P, 1], F32, name="neg_max")
-        nc.vector.tensor_reduce(neg_max[:], scores[:], AXIS.X, ALU.max, negate=True)
+        neg_scores = keep.tile([P, PACK, P // 2], F32, name="neg_scores")
+        nc.vector.tensor_scalar(
+            neg_scores[:], dealt[1], -1.0, neg_max_first[:], ALU.mult, ALU.min, accum_out=neg_max[:]
+        )
         group_share = keep.tile([P, 1], F32, name="group_share")
-        nc.vector.tensor_scalar(group_share[:], share_col[:], -float(G), float(G), ALU.mult, ALU.add)
+        nc.gpsimd.tensor_scalar(group_share[:], share_col[:], -float(G), float(G), ALU.mult, ALU.add)
 
         expo = keep.tile([P, 2, PACK, P // 2], F32, name="expo", align_bytes=64)
         half_sum = [keep.tile([P, 1], F32, name=f"half_sum{half}") for half in range(2)]
-        group_sum = keep.tile([P, G], F32, name="group_sum")
-        for half in range(2):
-            slots = slice(half * I // 2, (half + 1) * I // 2)
+        for half, (source, sign) in enumerate(((dealt[0], 1.0), (neg_scores[:], -1.0))):
             nc.scalar.activation(
                 expo[:, half, :, :],
-                scores[:, slots].rearrange("q (s t) -> q t s", t=PACK),
+                source,
                 ACT.Exp,
                 bias=neg_max[:],
+                scale=sign,
                 accum_out=half_sum[half][:],
             )
+        group_sum = keep.tile([P, 2, G // 2], F32, name="group_sum")
+        row_part = keep.tile([P, 1], F32, name="row_part")
+        mix = keep.tile([P, 2, G // 2], F32, name="mix")
+        inv_mix = keep.tile([P, 2, G // 2], F32, name="inv_mix")
+
+        def sum_groups(half):
             nc.vector.tensor_reduce(
-                group_sum[:, half * G // 2 : (half + 1) * G // 2],
+                group_sum[:, half, :],
                 expo[:, half, :, :].rearrange("q t (g h) -> q g t h", h=2),
                 AXIS.XY,
                 ALU.add,
             )
-        row_part = keep.tile([P, 1], F32, name="row_part")
+
+        sum_groups(0)
         nc.vector.tensor_scalar(
             row_part[:], half_sum[0][:], half_sum[1][:], share_col[:], ALU.add, ALU.mult
         )
-        mix = keep.tile([P, G], F32, name="mix")
-        nc.vector.tensor_scalar(mix[:], group_sum[:], group_share[:], row_part[:], ALU.mult, ALU.add)
-        inv_mix = keep.tile([P, G], F32, name="inv_mix")
-        nc.vector.reciprocal(inv_mix[:], mix[:])
-        weights = keep.tile([P, PACK, P], F32, name="weights", align_bytes=64)
+        sum_groups(1)
+        for half in range(2):
+            nc.vector.tensor_scalar(
+                mix[:, half, :], group_sum[:, half, :], group_share[:], row_part[:], ALU.mult, ALU.add
+            )
+        for half in range(2):
+            nc.vector.reciprocal(inv_mix[:, half, :], mix[:, half, :])
+
+        weights = keep.tile([P, PACK, 2, P // 2], F32, name="weights", align_bytes=64)
         weights_t = psum.tile([P, PACK, Q], F32, name="weights_t")
-        for u in range(2):
-            places = slice(2 * u, 2 * u + 2)
+
+        def weigh(places, halves):
+            n = halves.stop - halves.start
             nc.vector.tensor_tensor(
-                weights[:, places, :].rearrange("q t (a g h) -> q t a g h", a=2, h=2),
-                expo[:, :, places, :].rearrange("q a t (g h) -> q t a g h", h=2),
-                inv_mix[:]
-                .rearrange("q (a g) -> q a g", a=2)
-                .unsqueeze(1)
-                .unsqueeze(4)
-                .to_broadcast([P, 2, 2, G // 2, 2]),
+                weights[:, places, halves, :].rearrange("q t a (g h) -> q t a g h", h=2),
+                expo[:, halves, places, :].rearrange("q a t (g h) -> q t a g h", h=2),
+                inv_mix[:, halves, :].unsqueeze(1).unsqueeze(4).to_broadcast([P, 2, n, G // 2, 2]),
                 ALU.mult,
             )
-            for t in range(2 * u, 2 * u + 2):
-                nc.tensor.transpose(weights_t[:, t, :], weights[:, t, :], identity[:])
+
+        weigh(slice(0, 2), slice(0, 1))
+        weigh(slice(0, 2), slice(1, 2))
+        weigh(slice(2, 4), slice(0, 2))
+        for t in range(PACK):
+            nc.tensor.transpose(
+                weights_t[:, t, :], weights[:, t, :, :].rearrange("q a s -> q (a s)"), identity[:]
+            )
         w_bf = keep.tile([P, Q, PACK], BF16, name="w_bf", align_bytes=64)
         nc.vector.tensor_tensor(
             w_bf[:],
@@ -168,17 +189,14 @@ def tile_attend_mixednorm_kernel(tc, query, keys_words, keys_scales, share, fact
                 nc.tensor.transpose(pairs_t[:, u, :], pairs[:, u : I // 2 : 2], identity[:])
             return pairs_t
 
-        def weave(b, pairs_t, tag, copy):
-            v_bf = keep.tile([P, P * PACK], BF16, name=f"v_bf{b}", tag=tag, align_bytes=64)
+        def weave(v_bf, pairs_t, copy):
             copy(
                 v_bf[:].bitcast(F32).rearrange("s (e u) -> s e u", u=2),
                 pairs_t[:].rearrange("s u e -> s e u"),
             )
-            return v_bf
 
-        def product(first, v_bfs, codes_tag, bank_tag, copy):
+        def product(first, v_bfs, v_codes, bank_tag):
             n = len(v_bfs) * P
-            v_codes = keep.tile([P, n], U32, name=f"v_codes{first}", tag=codes_tag, align_bytes=64)
             v_scales = keep.tile([P, n], U8, name=f"v_scales{first}", align_bytes=64)
             for j, v_bf in enumerate(v_bfs):
                 nc.vector.quantize_mx(
@@ -196,16 +214,31 @@ def tile_attend_mixednorm_kernel(tc, query, keys_words, keys_scales, share, fact
                 start=True,
                 stop=True,
             )
-            result = keep.tile([P, n], F32, name=f"result{first}")
-            copy(result[:], acc[:])
-            nc.sync.dma_start(out[:, first * P : first * P + n], result[:])
+            return acc
 
-        v_bf0 = weave(0, pick(0), "expo", nc.vector.tensor_copy)
-        v_bf1 = weave(1, pick(1), "weights", nc.vector.tensor_copy)
+        def store(first, acc, result, copy):
+            copy(result[:], acc[:])
+            nc.sync.dma_start(out[:, first * P : first * P + result.shape[1]], result[:])
+
+        v_bf0 = keep.tile([P, I], BF16, name="v_bf0", tag="expo", align_bytes=64)
+        weave(v_bf0, pick(0), nc.vector.tensor_copy)
+        v_bf1 = keep.tile([P, I], BF16, name="v_bf1", tag="weights", align_bytes=64)
+        weave(v_bf1, pick(1), nc.vector.tensor_copy)
         pairs_t2 = pick(2)
-        product(0, [v_bf0, v_bf1], "w_bf", "scores", nc.scalar.copy)
         pairs_t3 = pick(3)
-        v_bf3 = weave(3, pairs_t3, "v_bf3", nc.scalar.copy)
-        v_bf2 = weave(2, pairs_t2, "val_pool3", nc.vector.tensor_copy)
-        product(2, [v_bf2], "v_codes2", "acc2", nc.scalar.copy)
-        product(3, [v_bf3], "v_codes3", "acc3", nc.vector.tensor_copy)
+        v_bf3 = keep.tile([P, I], BF16, name="v_bf3", align_bytes=64)
+        weave(v_bf3, pairs_t3, nc.scalar.copy)
+        v_bf2 = late.tile([P, I], BF16, name="v_bf2", align_bytes=64, offset=0)
+        weave(v_bf2, pairs_t2, nc.vector.tensor_copy)
+        v_codes0 = late.tile([P, 2 * P], U32, name="v_codes0", align_bytes=64, offset=2 * I)
+        acc0 = product(0, [v_bf0, v_bf1], v_codes0, "acc0")
+        v_codes2 = keep.tile([P, P], U32, name="v_codes2", align_bytes=64)
+        acc2 = product(2, [v_bf2], v_codes2, "acc1")
+        v_codes3 = keep.tile([P, P], U32, name="v_codes3", align_bytes=64)
+        acc3 = product(3, [v_bf3], v_codes3, "acc3")
+        result0 = late.tile([P, 2 * P], F32, name="result0", align_bytes=64, offset=0)
+        store(0, acc0, result0, nc.scalar.copy)
+        result2 = keep.tile([P, P], F32, name="result2")
+        store(2, acc2, result2, nc.scalar.copy)
+        result3 = keep.tile([P, P], F32, name="result3")
+        store(3, acc3, result3, nc.vector.tensor_copy)

@@ -230,13 +230,13 @@ def tile_attend_mixednorm_kernel(tc, query, keys_words, keys_scales, share, fact
         weave(v_bf3, pairs_t3, nc.scalar.copy)
         v_bf2 = late.tile([P, I], BF16, name="v_bf2", align_bytes=64, offset=0)
         weave(v_bf2, pairs_t2, nc.vector.tensor_copy)
-        v_codes0 = late.tile([P, 2 * P], U32, name="v_codes0", align_bytes=64, offset=2 * I)
+        v_codes0 = keep.tile([P, 2 * P], U32, name="v_codes0", tag="w_bf", align_bytes=64)
         acc0 = product(0, [v_bf0, v_bf1], v_codes0, "acc0")
         v_codes2 = keep.tile([P, P], U32, name="v_codes2", align_bytes=64)
         acc2 = product(2, [v_bf2], v_codes2, "acc1")
         v_codes3 = keep.tile([P, P], U32, name="v_codes3", align_bytes=64)
         acc3 = product(3, [v_bf3], v_codes3, "acc3")
-        result0 = late.tile([P, 2 * P], F32, name="result0", align_bytes=64, offset=0)
+        result0 = late.tile([P, 2 * P], F32, name="result0", align_bytes=64, offset=2 * I)
         store(0, acc0, result0, nc.scalar.copy)
         result2 = keep.tile([P, P], F32, name="result2")
         store(2, acc2, result2, nc.scalar.copy)

from contextlib import ExitStack

import concourse.mybir as mybir
from concourse.masks import make_identity

D, E, T, I, Q, G = 512, 512, 2048, 512, 128, 64
FLOPS = 2 * D * Q * I + 2 * I * Q * E

F32 = mybir.dt.float32
BF16 = mybir.dt.bfloat16
I32 = mybir.dt.int32
U32 = mybir.dt.uint32
U16 = mybir.dt.uint16
U8 = mybir.dt.uint8
FP8X4 = mybir.dt.float8_e4m3fn_x4
ALU = mybir.AluOpType
ACT = mybir.ActivationFunctionType
AXIS = mybir.AxisListType

P = 128
PACK = 4
BLOCKS = E // P
GROUP = I // G
LIST_COLS = I // 16
VECTOR_COLS = 18
KEY_HEAD = 512


def tile_attend_mixednorm_kernel(tc, query, keys_words, keys_scales, share, factors, vals, offs, out):
    nc = tc.nc
    with ExitStack() as ctx:
        lists = ctx.enter_context(tc.tile_pool(name="lists", bufs=1))
        keep = ctx.enter_context(tc.tile_pool(name="keep", bufs=1))
        late = ctx.enter_context(tc.tile_pool(name="late", bufs=1))
        psum = ctx.enter_context(tc.psum_pool(name="psum", bufs=1))

        key_scale_pool = keep.tile([P, T], U8, name="key_scale_pool", align_bytes=64)
        nc.vector.memset(key_scale_pool[:].bitcast(I32), 0)

        q_raw = keep.tile([P, PACK, Q], F32, name="q_raw")
        nc.sync.dma_start(q_raw[:], query.rearrange("(p j) q -> p j q", j=PACK))
        offsets = lists.tile([P, LIST_COLS], U16, name="offsets")
        nc.sync.dma_start(offsets[:], offs)
        key_word_pool = keep.tile([P, T], U32, name="key_word_pool", align_bytes=64)
        key_rows = keys_words[0].rearrange("p n t -> p (n t)").bitcast(I32)
        nc.sync.dma_start(key_word_pool[:, :KEY_HEAD].bitcast(I32), key_rows[:, :KEY_HEAD])
        for r in range(4):
            nc.sync.dma_start(
                key_scale_pool[r:P:32, :].bitcast(I32), keys_scales[0, r:16:4, :].bitcast(I32)
            )
        nc.sync.dma_start(key_word_pool[:, KEY_HEAD:].bitcast(I32), key_rows[:, KEY_HEAD:])
        slot_factor = keep.tile([P, PACK], F32, name="slot_factor")
        nc.sync.dma_start(slot_factor[:], factors.rearrange("o (p t) -> (o p) t", t=PACK))
        val_pool = [keep.tile([P, T], F32, name=f"val_pool{b}") for b in range(BLOCKS - 1)]
        val_pool.append(late.tile([P, T], F32, name="val_pool_last", align_bytes=64, offset=0))
        nc.sync.dma_start(val_pool[0][:], vals[0:P, :])

        for b in range(1, BLOCKS):
            nc.sync.dma_start(val_pool[b][:], vals[b * P : (b + 1) * P, :])
        share_col = keep.tile([P, 1], F32, name="share_col")
        nc.gpsimd.dma_start(share_col[:], share)

        identity = keep.tile([P, P], F32, name="identity")
        make_identity(nc, identity[:])

        q_bf = keep.tile([P, Q, PACK], BF16, name="q_bf", align_bytes=64)
        nc.vector.tensor_copy(q_bf[:], q_raw[:].rearrange("p j q -> p q j"))
        q_codes = keep.tile([P, Q], U32, name="q_codes", align_bytes=64)
        q_scales = keep.tile([P, Q], U8, name="q_scales", align_bytes=64)
        key_scales = keep.tile([P, I], U8, name="key_scales", align_bytes=64)
        nc.vector.tensor_copy(key_scales[:], key_scale_pool[:].indirect(offsets[:]))
        nc.vector.quantize_mx(
            out=q_codes[:].bitcast(FP8X4),
            scales=q_scales[:],
            in_=q_bf[:].rearrange("p q j -> p (q j)"),
        )
        key_words = keep.tile([P, I], U32, name="key_words", align_bytes=64)
        scores = [psum.tile([P, I // 2], F32, name=f"scores{half}", tag=f"acc{half}") for half in range(2)]
        for half in range(2):
            slots = slice(half * I // 2, (half + 1) * I // 2)
            cols = slice(half * LIST_COLS // 2, (half + 1) * LIST_COLS // 2)
            nc.vector.tensor_copy(key_words[:, slots], key_word_pool[:].indirect(offsets[:, cols]))
            nc.tensor.matmul_mx(
                out=scores[half][:],
                lhsT=q_codes[:].bitcast(FP8X4),
                lhsT_scale=q_scales[:],
                rhs=key_words[:, slots].bitcast(FP8X4),
                rhs_scale=key_scales[:, slots],
                start=True,
                stop=True,
            )
        dealt = [scores[half][:].rearrange("q (s t) -> q t s", t=PACK) for half in range(2)]

        neg_max_first = keep.tile([P, 1], F32, name="neg_max_first")
        nc.vector.tensor_reduce(neg_max_first[:], scores[0][:], AXIS.X, ALU.max, negate=True)
        neg_max = keep.tile([P, 1], F32, name="neg_max")
        neg_scores = keep.tile([P, PACK, P // 2], F32, name="neg_scores")
        nc.vector.tensor_scalar(
            neg_scores[:], dealt[1], -1.0, neg_max_first[:], ALU.mult, ALU.min, accum_out=neg_max[:]
        )
        group_share = keep.tile([P, 1], F32, name="group_share")
        nc.gpsimd.tensor_scalar(group_share[:], share_col[:], -float(G), float(G), ALU.mult, ALU.add)

        expo = keep.tile([P, 2, PACK, P // 2], F32, name="expo", align_bytes=64)
        half_sum = [keep.tile([P, 1], F32, name=f"half_sum{half}") for half in range(2)]
        for half, (source, sign) in enumerate(((dealt[0], 1.0), (neg_scores[:], -1.0))):
            nc.scalar.activation(
                expo[:, half, :, :],
                source,
                ACT.Exp,
                bias=neg_max[:],
                scale=sign,
                accum_out=half_sum[half][:],
            )
        group_sum = keep.tile([P, 2, G // 2], F32, name="group_sum")
        row_part = keep.tile([P, 1], F32, name="row_part")
        mix = keep.tile([P, 2, G // 2], F32, name="mix")
        inv_mix = keep.tile([P, 2, G // 2], F32, name="inv_mix")

        def sum_groups(half):
            nc.vector.tensor_reduce(
                group_sum[:, half, :],
                expo[:, half, :, :].rearrange("q t (g h) -> q g t h", h=2),
                AXIS.XY,
                ALU.add,
            )

        sum_groups(0)
        nc.vector.tensor_scalar(
            row_part[:], half_sum[0][:], half_sum[1][:], share_col[:], ALU.add, ALU.mult
        )
        sum_groups(1)
        for half in range(2):
            nc.vector.tensor_scalar(
                mix[:, half, :], group_sum[:, half, :], group_share[:], row_part[:], ALU.mult, ALU.add
            )
        for half in range(2):
            nc.vector.reciprocal(inv_mix[:, half, :], mix[:, half, :])

        weights = keep.tile([P, PACK, 2, P // 2], F32, name="weights", align_bytes=64)
        weights_t = psum.tile([P, PACK, Q], F32, name="weights_t")

        def weigh(places, halves):
            n = halves.stop - halves.start
            nc.vector.tensor_tensor(
                weights[:, places, halves, :].rearrange("q t a (g h) -> q t a g h", h=2),
                expo[:, halves, places, :].rearrange("q a t (g h) -> q t a g h", h=2),
                inv_mix[:, halves, :].unsqueeze(1).unsqueeze(4).to_broadcast([P, 2, n, G // 2, 2]),
                ALU.mult,
            )

        weigh(slice(0, 2), slice(0, 1))
        weigh(slice(0, 2), slice(1, 2))
        weigh(slice(2, 4), slice(0, 2))
        for t in range(PACK):
            nc.tensor.transpose(
                weights_t[:, t, :], weights[:, t, :, :].rearrange("q a s -> q (a s)"), identity[:]
            )
        w_bf = keep.tile([P, Q, PACK], BF16, name="w_bf", align_bytes=64)
        nc.vector.tensor_tensor(
            w_bf[:],
            weights_t[:].rearrange("s t q -> s q t"),
            slot_factor[:].unsqueeze(1).to_broadcast([P, Q, PACK]),
            ALU.mult,
        )
        w_codes = keep.tile([P, Q], U32, name="w_codes", align_bytes=64)
        w_scales = keep.tile([P, Q], U8, name="w_scales", align_bytes=64)
        nc.vector.quantize_mx(
            out=w_codes[:].bitcast(FP8X4),
            scales=w_scales[:],
            in_=w_bf[:].rearrange("s q t -> s (q t)"),
        )

        def pick(b):
            picked = keep.tile([P, I], BF16, name=f"picked{b}", align_bytes=64)
            if b < BLOCKS - 1:
                nc.scalar.activation(picked[:], val_pool[b][:].indirect(offsets[:]), ACT.Copy)
            else:
                cut = 16 * VECTOR_COLS
                nc.vector.tensor_copy(
                    picked[:, :cut], val_pool[b][:].indirect(offsets[:, :VECTOR_COLS])
                )
                nc.scalar.activation(
                    picked[:, cut:], val_pool[b][:].indirect(offsets[:, VECTOR_COLS:]), ACT.Copy
                )
            pairs = picked[:].bitcast(F32)
            pairs_t = psum.tile([P, 2, P], F32, name=f"pairs_t{b}")
            for u in range(2):
                nc.tensor.transpose(pairs_t[:, u, :], pairs[:, u : I // 2 : 2], identity[:])
            return pairs_t

        def weave(v_bf, pairs_t, copy):
            copy(
                v_bf[:].bitcast(F32).rearrange("s (e u) -> s e u", u=2),
                pairs_t[:].rearrange("s u e -> s e u"),
            )

        def product(first, v_bfs, v_codes, bank_tag):
            n = len(v_bfs) * P
            v_scales = keep.tile([P, n], U8, name=f"v_scales{first}", align_bytes=64)
            for j, v_bf in enumerate(v_bfs):
                nc.vector.quantize_mx(
                    out=v_codes[:, j * P : (j + 1) * P].bitcast(FP8X4),
                    scales=v_scales[:, j * P : (j + 1) * P],
                    in_=v_bf[:],
                )
            acc = psum.tile([P, n], F32, name=f"acc{first}", tag=bank_tag)
            nc.tensor.matmul_mx(
                out=acc[:],
                lhsT=w_codes[:].bitcast(FP8X4),
                lhsT_scale=w_scales[:],
                rhs=v_codes[:].bitcast(FP8X4),
                rhs_scale=v_scales[:],
                start=True,
                stop=True,
            )
            return acc

        def store(first, acc, result, copy):
            copy(result[:], acc[:])
            nc.sync.dma_start(out[:, first * P : first * P + result.shape[1]], result[:])

        v_bf0 = keep.tile([P, I], BF16, name="v_bf0", tag="expo", align_bytes=64)
        weave(v_bf0, pick(0), nc.vector.tensor_copy)
        v_bf1 = keep.tile([P, I], BF16, name="v_bf1", tag="weights", align_bytes=64)
        weave(v_bf1, pick(1), nc.vector.tensor_copy)
        pairs_t2 = pick(2)
        pairs_t3 = pick(3)
        v_bf3 = keep.tile([P, I], BF16, name="v_bf3", align_bytes=64)
        weave(v_bf3, pairs_t3, nc.scalar.copy)
        v_bf2 = late.tile([P, I], BF16, name="v_bf2", align_bytes=64, offset=0)
        weave(v_bf2, pairs_t2, nc.vector.tensor_copy)
        v_codes0 = keep.tile([P, 2 * P], U32, name="v_codes0", tag="w_bf", align_bytes=64)
        acc0 = product(0, [v_bf0, v_bf1], v_codes0, "acc0")
        v_codes2 = keep.tile([P, P], U32, name="v_codes2", align_bytes=64)
        acc2 = product(2, [v_bf2], v_codes2, "acc1")
        v_codes3 = keep.tile([P, P], U32, name="v_codes3", align_bytes=64)
        acc3 = product(3, [v_bf3], v_codes3, "acc3")
        result0 = late.tile([P, 2 * P], F32, name="result0", align_bytes=64, offset=2 * I)
        store(0, acc0, result0, nc.scalar.copy)
        result2 = keep.tile([P, P], F32, name="result2")
        store(2, acc2, result2, nc.scalar.copy)
        result3 = keep.tile([P, P], F32, name="result3")
        store(3, acc3, result3, nc.vector.tensor_copy)
